import numpy as np, ml_dtypes
CORES = [24,25,26,27,28,29,30,31,224,225,226,227,228,229,230,231]
N = 16
R, TK = 64, 128
def setup_inputs(rng):
    v = (rng.standard_normal((N, 128, R), dtype=np.float32) / np.float32(np.sqrt(128 * N))).astype(ml_dtypes.bfloat16)
    return {"x": rng.standard_normal((N, 128, TK), dtype=np.float32).astype(ml_dtypes.bfloat16), "v": v, "vt": v.transpose(0, 2, 1).copy()}
def setup_inputs_big(rng):
    d = setup_inputs(rng)
    for k in ("x",): d[k] = (d[k].astype(np.float32) * 1048576.0).astype(d[k].dtype)
    return d
def setup_inputs_small(rng):
    d = setup_inputs(rng)
    for k in ("x",): d[k] = (d[k].astype(np.float32) * (1 / 1048576.0)).astype(d[k].dtype)
    return d
def setup_inputs_apart(rng):
    d = setup_inputs(rng)
    f = (10.0 ** rng.permutation(np.linspace(-1.5, 1.5, N))).astype(np.float32).reshape(N, 1, 1)
    for k in ("x",): d[k] = (d[k].astype(np.float32) * f).astype(d[k].dtype)
    return d
def reference(x, v, vt):
    X, V, VT = x.astype(np.float64), v.astype(np.float64), vt.astype(np.float64)
    t = sum(V[j].T @ X[j] for j in range(N))
    return {"y": np.stack([X[r] - 2.0 * (VT[r].T @ t) for r in range(N)]).astype(ml_dtypes.bfloat16)}

@@ -1,0 +1,107 @@
+from concourse.bass import DstId, RemoteDMATransfer
+from concourse.mybir import AluOpType
+
+H = 64
+
+SCRATCH = {
+    "xs": ("sbuf", [128, 128], "bfloat16"),
+    "vs": ("sbuf", [128, H], "bfloat16"),
+    "vt2": ("sbuf", [128, 128], "bfloat16"),
+    "w2": ("sbuf", [128, 128], "bfloat16"),
+    "part": ("sbuf", [128, H], "bfloat16"),
+    "land": ("sbuf", [128, 8 * H], "bfloat16"),
+    "sown": ("sbuf", [128, H], "bfloat16"),
+    "soth": ("sbuf", [128, H], "bfloat16"),
+    "ys": ("sbuf", [128, 128], "bfloat16"),
+    "pt": ("psum", [128, 512], "float32"),
+    "pya": ("psum", [128, 512], "float32"),
+    "pyb": ("psum", [128, 512], "float32"),
+}
+SEMAPHORES = ["ldxv", "ldvt", "mm1", "pc", "sc", "arr", "own", "oth", "sent", "mma", "mmb", "vd", "st"]
+
+
+def _bits(mask):
+    return sum((mask >> e) & 1 for e in range(mask.bit_length()))
+
+
+def rank_program(g, core, T, topo):
+    if T.rank_of(core) is None:
+        return
+    S = T.sem
+
+    def same_chip(a, b):
+        return topo.host(a) == topo.host(b) and topo.chip(a) == topo.chip(b)
+
+    def dst_id(d):
+        rid, pid = topo.addr(d, core)
+        return DstId(rid=rid, pnc=pid)
+
+    mine = [c for c in T.cores if same_chip(c, core)]
+    far = [c for c in T.cores if not same_chip(c, core)]
+    ports = [c for c in mine if all(topo.may_write(c, d) for d in far)]
+    is_port = core in ports
+    slot = {c: T.land[:, i * H:(i + 1) * H] for i, c in enumerate(mine)}
+    on_mask = topo.mask(core, [c for c in mine if c != core][0])
+
+    g.sync.dma_start(T.xs[:], T.x[:, :]).then_inc(S.ldxv, 16)
+    g.scalar.dma_start(T.vs[:], T.v[:, :]).then_inc(S.ldxv, 16)
+    g.sync.dma_start(T.vt2[0:H, :], T.vt[:, :]).then_inc(S.ldvt, 16)
+    g.scalar.dma_start(T.vt2[H:128, :], T.vt[:, :]).then_inc(S.ldvt, 16)
+
+    g.tensor.wait_ge(S.ldxv, 32)
+    g.tensor.matmul(T.pt[0:H, 0:H], T.vs[:], T.xs[:, 0:H], True, True).then_inc(S.mm1, 1)
+    g.tensor.matmul(T.pt[H:128, 0:H], T.vs[:], T.xs[:, H:128], True, True).then_inc(S.mm1, 1)
+    g.vector.wait_ge(S.mm1, 2)
+    g.vector.tensor_copy(T.part[:], T.pt[:, 0:H]).then_inc(S.pc, 1)
+    g.vector.wait_ge(S.ldvt, 32)
+    g.vector.tensor_tensor(T.w2[:], T.vt2[:], T.vt2[:], AluOpType.add).then_inc(S.sc, 1)
+
+    to = [p for p in ports if p != core]
+    g.wait_ge(S.pc, 1)
+    g.remote_dma_fused([RemoteDMATransfer(dst_ids=[dst_id(p) for p in to], dma_engine_mask=on_mask, remote_sem=S.arr,
+                                          srcs=[T.part[:]], dsts=[slot[core]] * len(to), alu_op=0)], local_sem=S.sent)
+    sent = _bits(on_mask)
+    n_arr = (len(mine) - 1) * _bits(on_mask)
+
+    off_mask = topo.mask(ports[0], far[0])
+    rest_mask = on_mask & ~off_mask
+    if is_port:
+        tiles = [T.part[:]] + [slot[c] for c in mine if c != core]
+        peers = [q for q in ports if topo.die(q) == topo.die(core)]
+        k = peers.index(core)
+        fd = [d for d in far if topo.die(d) == topo.die(core)][k::len(peers)]
+        nd = [d for d in mine if d not in ports and topo.die(d) == topo.die(core)][k::len(peers)]
+        g.wait_ge(S.arr, n_arr)
+        g.remote_dma_fused([
+            RemoteDMATransfer(dst_ids=[dst_id(d) for d in fd], dma_engine_mask=off_mask, remote_sem=S.oth,
+                              srcs=tiles, dsts=[T.soth[:]] * len(fd), alu_op=1),
+            RemoteDMATransfer(dst_ids=[dst_id(d) for d in nd], dma_engine_mask=rest_mask, remote_sem=S.own,
+                              srcs=tiles, dsts=[T.sown[:]] * len(nd), alu_op=1),
+        ], local_sem=S.sent)
+        sent += _bits(off_mask) + _bits(rest_mask)
+
+    g.tensor.wait_ge(S.sc, 1)
+    if is_port:
+        g.tensor.wait_ge(S.pc, 1)
+        g.tensor.wait_ge(S.arr, n_arr)
+        halves = [(T.part[0:H, :], T.part[H:128, :])]
+        halves += [(T.land[0:H, i * H:(i + 1) * H], T.land[H:128, i * H:(i + 1) * H])
+                   for i, c in enumerate(mine) if c != core]
+    else:
+        g.tensor.wait_ge(S.own, _bits(rest_mask))
+        halves = [(T.sown[0:H, :], T.sown[H:128, :])]
+    for i, (top, bot) in enumerate(halves):
+        g.tensor.matmul(T.pya[:, 0:H], T.w2[0:H, :], top, i == 0, False)
+        g.tensor.matmul(T.pyb[:, 0:H], T.w2[H:128, :], bot, i == 0, False)
+    g.tensor.wait_ge(S.oth, _bits(off_mask))
+    g.tensor.matmul(T.pya[:, 0:H], T.w2[0:H, :], T.soth[0:H, :], False, True).then_inc(S.mma, 1)
+    g.tensor.matmul(T.pyb[:, 0:H], T.w2[H:128, :], T.soth[H:128, :], False, True).then_inc(S.mmb, 1)
+
+    g.vector.wait_ge(S.mma, 1)
+    g.vector.tensor_tensor(T.ys[:, 0:H], T.xs[:, 0:H], T.pya[:, 0:H], AluOpType.subtract).then_inc(S.vd, 1)
+    g.vector.wait_ge(S.mmb, 1)
+    g.vector.tensor_tensor(T.ys[:, H:128], T.xs[:, H:128], T.pyb[:, 0:H], AluOpType.subtract).then_inc(S.vd, 1)
+    g.sync.wait_ge(S.vd, 2)
+    g.sync.dma_start(T.y[:, :], T.ys[:]).then_inc(S.st, 16)
+    g.sync.wait_ge(S.st, 16)
+    g.wait_ge(S.sent, sent)

@@ -8,16 +8,21 @@ SCRATCH = {
     "vs": ("sbuf", [128, H], "bfloat16"),
     "vt2": ("sbuf", [128, 128], "bfloat16"),
     "w2": ("sbuf", [128, 128], "bfloat16"),
+    "ones": ("sbuf", [128, 128], "bfloat16"),
+    "ident": ("sbuf", [128, 128], "bfloat16"),
     "part": ("sbuf", [128, H], "bfloat16"),
     "land": ("sbuf", [128, 8 * H], "bfloat16"),
+    "pre": ("sbuf", [128, H], "bfloat16"),
     "sown": ("sbuf", [128, H], "bfloat16"),
     "soth": ("sbuf", [128, H], "bfloat16"),
     "ys": ("sbuf", [128, 128], "bfloat16"),
     "pt": ("psum", [128, 512], "float32"),
+    "ps": ("psum", [128, 512], "float32"),
     "pya": ("psum", [128, 512], "float32"),
     "pyb": ("psum", [128, 512], "float32"),
 }
-SEMAPHORES = ["ldxv", "ldvt", "mm1", "pc", "sc", "arr", "own", "oth", "sent", "mma", "mmb", "vd", "st"]
+SEMAPHORES = ["ldxv", "ldvt", "mm1", "pc", "sc", "on", "idn", "sm", "cs", "la", "own", "oth", "sent", "mma", "mmb", "vd",
+              "st"] + ["a%d" % i for i in range(8)]
 
 
 def _bits(mask):
@@ -42,11 +47,29 @@ def rank_program(g, core, T, topo):
     is_port = core in ports
     slot = {c: T.land[:, i * H:(i + 1) * H] for i, c in enumerate(mine)}
     on_mask = topo.mask(core, [c for c in mine if c != core][0])
+    off_mask = topo.mask(ports[0], far[0])
+    rest_mask = on_mask & ~off_mask
+    n_off, n_rest = _bits(off_mask), _bits(rest_mask)
+
+    n_p = len(ports)
+    shift = [h for h in range(n_p) if all(ports[(i + h) % n_p] != s for i, s in enumerate(mine))][0]
+
+    def late_dst(s):
+        return ports[(mine.index(s) + shift) % n_p]
+
+    def early_dsts(s):
+        k = ports.index(late_dst(s))
+        return [p for p in ports[k + 1:] + ports[:k] if p != s]
 
     g.sync.dma_start(T.xs[:], T.x[:, :]).then_inc(S.ldxv, 16)
     g.scalar.dma_start(T.vs[:], T.v[:, :]).then_inc(S.ldxv, 16)
     g.sync.dma_start(T.vt2[0:H, :], T.vt[:, :]).then_inc(S.ldvt, 16)
     g.scalar.dma_start(T.vt2[H:128, :], T.vt[:, :]).then_inc(S.ldvt, 16)
+
+    if is_port:
+        g.vector.memset(T.ones[:], 1.0).then_inc(S.on, 1)
+        g.wait_ge(S.on, 1)
+        g.affine_select(T.ident[:], T.ones[:], [[-1, 128]], AluOpType.is_equal, 0.0, 0, 1).then_inc(S.idn, 1)
 
     g.tensor.wait_ge(S.ldxv, 32)
     g.tensor.matmul(T.pt[0:H, 0:H], T.vs[:], T.xs[:, 0:H], True, True).then_inc(S.mm1, 1)
@@ -56,44 +79,60 @@ def rank_program(g, core, T, topo):
     g.vector.wait_ge(S.ldvt, 32)
     g.vector.tensor_tensor(T.w2[:], T.vt2[:], T.vt2[:], AluOpType.add).then_inc(S.sc, 1)
 
-    to = [p for p in ports if p != core]
+    to = early_dsts(core)
     g.wait_ge(S.pc, 1)
-    g.remote_dma_fused([RemoteDMATransfer(dst_ids=[dst_id(p) for p in to], dma_engine_mask=on_mask, remote_sem=S.arr,
+    g.remote_dma_fused([RemoteDMATransfer(dst_ids=[dst_id(p) for p in to], dma_engine_mask=off_mask,
+                                          remote_sem=S["a%d" % mine.index(core)],
                                           srcs=[T.part[:]], dsts=[slot[core]] * len(to), alu_op=0)], local_sem=S.sent)
-    sent = _bits(on_mask)
-    n_arr = (len(mine) - 1) * _bits(on_mask)
+    g.remote_dma_fused([RemoteDMATransfer(dst_ids=[dst_id(late_dst(core))], dma_engine_mask=rest_mask, remote_sem=S.la,
+                                          srcs=[T.part[:]], dsts=[slot[core]], alu_op=0)], local_sem=S.sent)
+    sent = n_off + n_rest
 
-    off_mask = topo.mask(ports[0], far[0])
-    rest_mask = on_mask & ~off_mask
     if is_port:
-        tiles = [T.part[:]] + [slot[c] for c in mine if c != core]
+        late = [s for s in mine if late_dst(s) == core]
+        n_la = len(late) * n_rest
+        due = sorted([s for s in mine if s != core and s not in late],
+                     key=lambda s: (early_dsts(s).index(core), mine.index(s)))
+        g.tensor.wait_ge(S.idn, 1)
+        g.tensor.wait_ge(S.pc, 1)
+        g.tensor.matmul(T.ps[:, 0:H], T.ident[:], T.part[:], True, False)
+        for c in due[:-1]:
+            g.tensor.wait_ge(S["a%d" % mine.index(c)], n_off)
+            mm = g.tensor.matmul(T.ps[:, 0:H], T.ident[:], slot[c], False, c == due[-2])
+        mm.then_inc(S.sm, 1)
+        g.vector.wait_ge(S.sm, 1)
+        g.vector.wait_ge(S["a%d" % mine.index(due[-1])], n_off)
+        g.vector.tensor_tensor(T.pre[:], T.ps[:, 0:H], slot[due[-1]], AluOpType.add).then_inc(S.cs, 1)
+
+        tiles = [T.pre[:]] + [slot[s] for s in late]
         peers = [q for q in ports if topo.die(q) == topo.die(core)]
         k = peers.index(core)
         fd = [d for d in far if topo.die(d) == topo.die(core)][k::len(peers)]
         nd = [d for d in mine if d not in ports and topo.die(d) == topo.die(core)][k::len(peers)]
-        g.wait_ge(S.arr, n_arr)
+        g.wait_ge(S.cs, 1)
+        g.wait_ge(S.la, n_la)
         g.remote_dma_fused([
             RemoteDMATransfer(dst_ids=[dst_id(d) for d in fd], dma_engine_mask=off_mask, remote_sem=S.oth,
                               srcs=tiles, dsts=[T.soth[:]] * len(fd), alu_op=1),
             RemoteDMATransfer(dst_ids=[dst_id(d) for d in nd], dma_engine_mask=rest_mask, remote_sem=S.own,
                               srcs=tiles, dsts=[T.sown[:]] * len(nd), alu_op=1),
         ], local_sem=S.sent)
-        sent += _bits(off_mask) + _bits(rest_mask)
+        sent += n_off + n_rest
 
     g.tensor.wait_ge(S.sc, 1)
     if is_port:
-        g.tensor.wait_ge(S.pc, 1)
-        g.tensor.wait_ge(S.arr, n_arr)
-        halves = [(T.part[0:H, :], T.part[H:128, :])]
+        g.tensor.wait_ge(S.cs, 1)
+        g.tensor.wait_ge(S.la, n_la)
+        halves = [(T.pre[0:H, :], T.pre[H:128, :])]
         halves += [(T.land[0:H, i * H:(i + 1) * H], T.land[H:128, i * H:(i + 1) * H])
-                   for i, c in enumerate(mine) if c != core]
+                   for i, c in enumerate(mine) if c in late]
     else:
-        g.tensor.wait_ge(S.own, _bits(rest_mask))
+        g.tensor.wait_ge(S.own, n_rest)
         halves = [(T.sown[0:H, :], T.sown[H:128, :])]
     for i, (top, bot) in enumerate(halves):
         g.tensor.matmul(T.pya[:, 0:H], T.w2[0:H, :], top, i == 0, False)
         g.tensor.matmul(T.pyb[:, 0:H], T.w2[H:128, :], bot, i == 0, False)
-    g.tensor.wait_ge(S.oth, _bits(off_mask))
+    g.tensor.wait_ge(S.oth, n_off)
     g.tensor.matmul(T.pya[:, 0:H], T.w2[0:H, :], T.soth[0:H, :], False, True).then_inc(S.mma, 1)
     g.tensor.matmul(T.pyb[:, 0:H], T.w2[H:128, :], T.soth[H:128, :], False, True).then_inc(S.mmb, 1)
 

@@ -2,15 +2,16 @@ from concourse.bass import DstId, RemoteDMATransfer
 from concourse.mybir import AluOpType
 
 H = 64
+W = 192
 
 SCRATCH = {
-    "xs": ("sbuf", [128, 128], "bfloat16"),
-    "vs": ("sbuf", [128, H], "bfloat16"),
+    "xv": ("sbuf", [128, W], "bfloat16"),
     "vt2": ("sbuf", [128, 128], "bfloat16"),
     "w2": ("sbuf", [128, 128], "bfloat16"),
-    "ones": ("sbuf", [128, 128], "bfloat16"),
+    "ramp": ("sbuf", [128, 128], "bfloat16"),
     "ident": ("sbuf", [128, 128], "bfloat16"),
     "part": ("sbuf", [128, H], "bfloat16"),
+    "rland": ("sbuf", [128, 2 * W], "bfloat16"),
     "land": ("sbuf", [128, 8 * H], "bfloat16"),
     "pre": ("sbuf", [128, H], "bfloat16"),
     "sown": ("sbuf", [128, H], "bfloat16"),
@@ -21,8 +22,8 @@ SCRATCH = {
     "pya": ("psum", [128, 512], "float32"),
     "pyb": ("psum", [128, 512], "float32"),
 }
-SEMAPHORES = ["ldxv", "ldvt", "mm1", "pc", "sc", "on", "idn", "sm", "cs", "la", "own", "oth", "sent", "mma", "mmb", "vd",
-              "st"] + ["a%d" % i for i in range(8)]
+SEMAPHORES = ["ldxv", "ldvt", "mm1", "pc", "sc", "rmp", "idn", "sm", "cs", "ra", "la", "own", "oth", "sent", "mma", "mmb",
+              "vd", "st"] + ["a%d" % i for i in range(8)]
 
 
 def _bits(mask):
@@ -49,31 +50,47 @@ def rank_program(g, core, T, topo):
     on_mask = topo.mask(core, [c for c in mine if c != core][0])
     off_mask = topo.mask(ports[0], far[0])
     rest_mask = on_mask & ~off_mask
-    n_off, n_rest = _bits(off_mask), _bits(rest_mask)
+    rest = [e for e in range(rest_mask.bit_length()) if (rest_mask >> e) & 1]
+    raw_mask = sum(1 << e for e in rest[:len(rest) // 2])
+    late_mask = rest_mask & ~raw_mask
+    n_off, n_rest, n_raw, n_late = _bits(off_mask), _bits(rest_mask), _bits(raw_mask), _bits(late_mask)
 
     n_p = len(ports)
-    shift = [h for h in range(n_p) if all(ports[(i + h) % n_p] != s for i, s in enumerate(mine))][0]
+    ok = [h for h in range(n_p) if all(ports[(i + h) % n_p] != s for i, s in enumerate(mine))]
+
+    def raw_dst(s):
+        return ports[(mine.index(s) + ok[0]) % n_p]
 
     def late_dst(s):
-        return ports[(mine.index(s) + shift) % n_p]
+        return ports[(mine.index(s) + ok[1]) % n_p]
 
     def early_dsts(s):
         k = ports.index(late_dst(s))
-        return [p for p in ports[k + 1:] + ports[:k] if p != s]
+        return [p for p in ports[k + 1:] + ports[:k] if p != s and p != raw_dst(s)]
 
-    g.sync.dma_start(T.xs[:], T.x[:, :]).then_inc(S.ldxv, 16)
-    g.scalar.dma_start(T.vs[:], T.v[:, :]).then_inc(S.ldxv, 16)
+    def raw_of(p):
+        return [s for s in mine if raw_dst(s) == p]
+
+    g.sync.dma_start(T.xv[:, 0:128], T.x[:, :]).then_inc(S.ldxv, 16)
+    g.scalar.dma_start(T.xv[:, 128:W], T.v[:, :]).then_inc(S.ldxv, 16)
     g.sync.dma_start(T.vt2[0:H, :], T.vt[:, :]).then_inc(S.ldvt, 16)
     g.scalar.dma_start(T.vt2[H:128, :], T.vt[:, :]).then_inc(S.ldvt, 16)
 
     if is_port:
-        g.vector.memset(T.ones[:], 1.0).then_inc(S.on, 1)
-        g.wait_ge(S.on, 1)
-        g.affine_select(T.ident[:], T.ones[:], [[-1, 128]], AluOpType.is_equal, 0.0, 0, 1).then_inc(S.idn, 1)
+        g.iota(T.ramp[:], [[-1, 128]], 0, 1, allow_small_or_imprecise_dtypes=True).then_inc(S.rmp, 1)
+        g.vector.wait_ge(S.rmp, 1)
+        g.vector.tensor_scalar(T.ident[:], T.ramp[:], 0.0, None, AluOpType.is_equal).then_inc(S.idn, 1)
+
+    rd = raw_dst(core)
+    j = raw_of(rd).index(core)
+    g.wait_ge(S.ldxv, 32)
+    g.remote_dma_fused([RemoteDMATransfer(dst_ids=[dst_id(rd)], dma_engine_mask=raw_mask, remote_sem=S.ra,
+                                          srcs=[T.xv[:]], dsts=[T.rland[:, j * W:(j + 1) * W]], alu_op=0)],
+                       local_sem=S.sent)
 
     g.tensor.wait_ge(S.ldxv, 32)
-    g.tensor.matmul(T.pt[0:H, 0:H], T.vs[:], T.xs[:, 0:H], True, True).then_inc(S.mm1, 1)
-    g.tensor.matmul(T.pt[H:128, 0:H], T.vs[:], T.xs[:, H:128], True, True).then_inc(S.mm1, 1)
+    g.tensor.matmul(T.pt[0:H, 0:H], T.xv[:, 128:W], T.xv[:, 0:H], True, True).then_inc(S.mm1, 1)
+    g.tensor.matmul(T.pt[H:128, 0:H], T.xv[:, 128:W], T.xv[:, H:128], True, True).then_inc(S.mm1, 1)
     g.vector.wait_ge(S.mm1, 2)
     g.vector.tensor_copy(T.part[:], T.pt[:, 0:H]).then_inc(S.pc, 1)
     g.vector.wait_ge(S.ldvt, 32)
@@ -84,18 +101,24 @@ def rank_program(g, core, T, topo):
     g.remote_dma_fused([RemoteDMATransfer(dst_ids=[dst_id(p) for p in to], dma_engine_mask=off_mask,
                                           remote_sem=S["a%d" % mine.index(core)],
                                           srcs=[T.part[:]], dsts=[slot[core]] * len(to), alu_op=0)], local_sem=S.sent)
-    g.remote_dma_fused([RemoteDMATransfer(dst_ids=[dst_id(late_dst(core))], dma_engine_mask=rest_mask, remote_sem=S.la,
+    g.remote_dma_fused([RemoteDMATransfer(dst_ids=[dst_id(late_dst(core))], dma_engine_mask=late_mask, remote_sem=S.la,
                                           srcs=[T.part[:]], dsts=[slot[core]], alu_op=0)], local_sem=S.sent)
-    sent = n_off + n_rest
+    sent = n_raw + n_off + n_late
 
     if is_port:
         late = [s for s in mine if late_dst(s) == core]
-        n_la = len(late) * n_rest
-        due = sorted([s for s in mine if s != core and s not in late],
+        raws = raw_of(core)
+        n_la = len(late) * n_late
+        due = sorted([s for s in mine if s != core and s not in late and s not in raws],
                      key=lambda s: (early_dsts(s).index(core), mine.index(s)))
         g.tensor.wait_ge(S.idn, 1)
         g.tensor.wait_ge(S.pc, 1)
         g.tensor.matmul(T.ps[:, 0:H], T.ident[:], T.part[:], True, False)
+        g.tensor.wait_ge(S.ra, len(raws) * n_raw)
+        for n in range(len(raws)):
+            b = n * W
+            g.tensor.matmul(T.ps[0:H, 0:H], T.rland[:, b + 128:b + W], T.rland[:, b:b + H], False, False)
+            g.tensor.matmul(T.ps[H:128, 0:H], T.rland[:, b + 128:b + W], T.rland[:, b + H:b + 128], False, False)
         for c in due[:-1]:
             g.tensor.wait_ge(S["a%d" % mine.index(c)], n_off)
             mm = g.tensor.matmul(T.ps[:, 0:H], T.ident[:], slot[c], False, c == due[-2])
@@ -137,9 +160,9 @@ def rank_program(g, core, T, topo):
     g.tensor.matmul(T.pyb[:, 0:H], T.w2[H:128, :], T.soth[H:128, :], False, True).then_inc(S.mmb, 1)
 
     g.vector.wait_ge(S.mma, 1)
-    g.vector.tensor_tensor(T.ys[:, 0:H], T.xs[:, 0:H], T.pya[:, 0:H], AluOpType.subtract).then_inc(S.vd, 1)
+    g.vector.tensor_tensor(T.ys[:, 0:H], T.xv[:, 0:H], T.pya[:, 0:H], AluOpType.subtract).then_inc(S.vd, 1)
     g.vector.wait_ge(S.mmb, 1)
-    g.vector.tensor_tensor(T.ys[:, H:128], T.xs[:, H:128], T.pyb[:, 0:H], AluOpType.subtract).then_inc(S.vd, 1)
+    g.vector.tensor_tensor(T.ys[:, H:128], T.xv[:, H:128], T.pyb[:, 0:H], AluOpType.subtract).then_inc(S.vd, 1)
     g.sync.wait_ge(S.vd, 2)
     g.sync.dma_start(T.y[:, :], T.ys[:]).then_inc(S.st, 16)
     g.sync.wait_ge(S.st, 16)

from concourse.bass import DstId, RemoteDMATransfer
from concourse.mybir import AluOpType

H = 64
W = 192

SCRATCH = {
    "xv": ("sbuf", [128, W], "bfloat16"),
    "vt2": ("sbuf", [128, 128], "bfloat16"),
    "w2": ("sbuf", [128, 128], "bfloat16"),
    "ramp": ("sbuf", [128, 128], "bfloat16"),
    "ident": ("sbuf", [128, 128], "bfloat16"),
    "part": ("sbuf", [128, H], "bfloat16"),
    "rland": ("sbuf", [128, 2 * W], "bfloat16"),
    "land": ("sbuf", [128, 8 * H], "bfloat16"),
    "pre": ("sbuf", [128, H], "bfloat16"),
    "sown": ("sbuf", [128, H], "bfloat16"),
    "soth": ("sbuf", [128, H], "bfloat16"),
    "ys": ("sbuf", [128, 128], "bfloat16"),
    "pt": ("psum", [128, 512], "float32"),
    "ps": ("psum", [128, 512], "float32"),
    "pya": ("psum", [128, 512], "float32"),
    "pyb": ("psum", [128, 512], "float32"),
}
SEMAPHORES = ["ldxv", "ldvt", "mm1", "pc", "sc", "rmp", "idn", "sm", "cs", "ra", "la", "own", "oth", "sent", "mma", "mmb",
              "vd", "st"] + ["a%d" % i for i in range(8)]


def _bits(mask):
    return sum((mask >> e) & 1 for e in range(mask.bit_length()))


def rank_program(g, core, T, topo):
    if T.rank_of(core) is None:
        return
    S = T.sem

    def same_chip(a, b):
        return topo.host(a) == topo.host(b) and topo.chip(a) == topo.chip(b)

    def dst_id(d):
        rid, pid = topo.addr(d, core)
        return DstId(rid=rid, pnc=pid)

    mine = [c for c in T.cores if same_chip(c, core)]
    far = [c for c in T.cores if not same_chip(c, core)]
    ports = [c for c in mine if all(topo.may_write(c, d) for d in far)]
    is_port = core in ports
    slot = {c: T.land[:, i * H:(i + 1) * H] for i, c in enumerate(mine)}
    on_mask = topo.mask(core, [c for c in mine if c != core][0])
    off_mask = topo.mask(ports[0], far[0])
    rest_mask = on_mask & ~off_mask
    rest = [e for e in range(rest_mask.bit_length()) if (rest_mask >> e) & 1]
    raw_mask = sum(1 << e for e in rest[:len(rest) // 2])
    late_mask = rest_mask & ~raw_mask
    n_off, n_rest, n_raw, n_late = _bits(off_mask), _bits(rest_mask), _bits(raw_mask), _bits(late_mask)

    n_p = len(ports)
    ok = [h for h in range(n_p) if all(ports[(i + h) % n_p] != s for i, s in enumerate(mine))]

    def raw_dst(s):
        return ports[(mine.index(s) + ok[0]) % n_p]

    def late_dst(s):
        return ports[(mine.index(s) + ok[1]) % n_p]

    def early_dsts(s):
        k = ports.index(late_dst(s))
        return [p for p in ports[k + 1:] + ports[:k] if p != s and p != raw_dst(s)]

    def raw_of(p):
        return [s for s in mine if raw_dst(s) == p]

    g.sync.dma_start(T.xv[:, 0:128], T.x[:, :]).then_inc(S.ldxv, 16)
    g.scalar.dma_start(T.xv[:, 128:W], T.v[:, :]).then_inc(S.ldxv, 16)
    g.sync.dma_start(T.vt2[0:H, :], T.vt[:, :]).then_inc(S.ldvt, 16)
    g.scalar.dma_start(T.vt2[H:128, :], T.vt[:, :]).then_inc(S.ldvt, 16)

    if is_port:
        g.iota(T.ramp[:], [[-1, 128]], 0, 1, allow_small_or_imprecise_dtypes=True).then_inc(S.rmp, 1)
        g.vector.wait_ge(S.rmp, 1)
        g.vector.tensor_scalar(T.ident[:], T.ramp[:], 0.0, None, AluOpType.is_equal).then_inc(S.idn, 1)

    rd = raw_dst(core)
    j = raw_of(rd).index(core)
    g.wait_ge(S.ldxv, 32)
    g.remote_dma_fused([RemoteDMATransfer(dst_ids=[dst_id(rd)], dma_engine_mask=raw_mask, remote_sem=S.ra,
                                          srcs=[T.xv[:]], dsts=[T.rland[:, j * W:(j + 1) * W]], alu_op=0)],
                       local_sem=S.sent)

    g.tensor.wait_ge(S.ldxv, 32)
    g.tensor.matmul(T.pt[0:H, 0:H], T.xv[:, 128:W], T.xv[:, 0:H], True, True).then_inc(S.mm1, 1)
    g.tensor.matmul(T.pt[H:128, 0:H], T.xv[:, 128:W], T.xv[:, H:128], True, True).then_inc(S.mm1, 1)
    g.vector.wait_ge(S.mm1, 2)
    g.vector.tensor_copy(T.part[:], T.pt[:, 0:H]).then_inc(S.pc, 1)
    g.vector.wait_ge(S.ldvt, 32)
    g.vector.tensor_tensor(T.w2[:], T.vt2[:], T.vt2[:], AluOpType.add).then_inc(S.sc, 1)

    to = early_dsts(core)
    g.wait_ge(S.pc, 1)
    g.remote_dma_fused([RemoteDMATransfer(dst_ids=[dst_id(p) for p in to], dma_engine_mask=off_mask,
                                          remote_sem=S["a%d" % mine.index(core)],
                                          srcs=[T.part[:]], dsts=[slot[core]] * len(to), alu_op=0)], local_sem=S.sent)
    g.remote_dma_fused([RemoteDMATransfer(dst_ids=[dst_id(late_dst(core))], dma_engine_mask=late_mask, remote_sem=S.la,
                                          srcs=[T.part[:]], dsts=[slot[core]], alu_op=0)], local_sem=S.sent)
    sent = n_raw + n_off + n_late

    if is_port:
        late = [s for s in mine if late_dst(s) == core]
        raws = raw_of(core)
        n_la = len(late) * n_late
        due = sorted([s for s in mine if s != core and s not in late and s not in raws],
                     key=lambda s: (early_dsts(s).index(core), mine.index(s)))
        g.tensor.wait_ge(S.idn, 1)
        g.tensor.wait_ge(S.pc, 1)
        g.tensor.matmul(T.ps[:, 0:H], T.ident[:], T.part[:], True, False)
        g.tensor.wait_ge(S.ra, len(raws) * n_raw)
        for n in range(len(raws)):
            b = n * W
            g.tensor.matmul(T.ps[0:H, 0:H], T.rland[:, b + 128:b + W], T.rland[:, b:b + H], False, False)
            g.tensor.matmul(T.ps[H:128, 0:H], T.rland[:, b + 128:b + W], T.rland[:, b + H:b + 128], False, False)
        for c in due[:-1]:
            g.tensor.wait_ge(S["a%d" % mine.index(c)], n_off)
            mm = g.tensor.matmul(T.ps[:, 0:H], T.ident[:], slot[c], False, c == due[-2])
        mm.then_inc(S.sm, 1)
        g.vector.wait_ge(S.sm, 1)
        g.vector.wait_ge(S["a%d" % mine.index(due[-1])], n_off)
        g.vector.tensor_tensor(T.pre[:], T.ps[:, 0:H], slot[due[-1]], AluOpType.add).then_inc(S.cs, 1)

        tiles = [T.pre[:]] + [slot[s] for s in late]
        peers = [q for q in ports if topo.die(q) == topo.die(core)]
        k = peers.index(core)
        fd = [d for d in far if topo.die(d) == topo.die(core)][k::len(peers)]
        nd = [d for d in mine if d not in ports and topo.die(d) == topo.die(core)][k::len(peers)]
        g.wait_ge(S.cs, 1)
        g.wait_ge(S.la, n_la)
        g.remote_dma_fused([
            RemoteDMATransfer(dst_ids=[dst_id(d) for d in fd], dma_engine_mask=off_mask, remote_sem=S.oth,
                              srcs=tiles, dsts=[T.soth[:]] * len(fd), alu_op=1),
            RemoteDMATransfer(dst_ids=[dst_id(d) for d in nd], dma_engine_mask=rest_mask, remote_sem=S.own,
                              srcs=tiles, dsts=[T.sown[:]] * len(nd), alu_op=1),
        ], local_sem=S.sent)
        sent += n_off + n_rest

    g.tensor.wait_ge(S.sc, 1)
    if is_port:
        g.tensor.wait_ge(S.cs, 1)
        g.tensor.wait_ge(S.la, n_la)
        halves = [(T.pre[0:H, :], T.pre[H:128, :])]
        halves += [(T.land[0:H, i * H:(i + 1) * H], T.land[H:128, i * H:(i + 1) * H])
                   for i, c in enumerate(mine) if c in late]
    else:
        g.tensor.wait_ge(S.own, n_rest)
        halves = [(T.sown[0:H, :], T.sown[H:128, :])]
    for i, (top, bot) in enumerate(halves):
        g.tensor.matmul(T.pya[:, 0:H], T.w2[0:H, :], top, i == 0, False)
        g.tensor.matmul(T.pyb[:, 0:H], T.w2[H:128, :], bot, i == 0, False)
    g.tensor.wait_ge(S.oth, n_off)
    g.tensor.matmul(T.pya[:, 0:H], T.w2[0:H, :], T.soth[0:H, :], False, True).then_inc(S.mma, 1)
    g.tensor.matmul(T.pyb[:, 0:H], T.w2[H:128, :], T.soth[H:128, :], False, True).then_inc(S.mmb, 1)

    g.vector.wait_ge(S.mma, 1)
    g.vector.tensor_tensor(T.ys[:, 0:H], T.xv[:, 0:H], T.pya[:, 0:H], AluOpType.subtract).then_inc(S.vd, 1)
    g.vector.wait_ge(S.mmb, 1)
    g.vector.tensor_tensor(T.ys[:, H:128], T.xv[:, H:128], T.pyb[:, 0:H], AluOpType.subtract).then_inc(S.vd, 1)
    g.sync.wait_ge(S.vd, 2)
    g.sync.dma_start(T.y[:, :], T.ys[:]).then_inc(S.st, 16)
    g.sync.wait_ge(S.st, 16)
    g.wait_ge(S.sent, sent)
